import numpy as np
import ml_dtypes


def mxq(x, axis, fmt="e4m3"):
    dtype, down = {"e4m3": (ml_dtypes.float8_e4m3fn, 7), "e5m2": (ml_dtypes.float8_e5m2, 14)}[fmt]
    v = np.moveaxis(np.asarray(x, np.float32).astype(ml_dtypes.bfloat16).astype(np.float64), axis, -1)
    blocks = v.reshape(v.shape[:-1] + (-1, 32))
    amax = np.abs(blocks).max(-1, keepdims=True)
    byte = np.maximum(np.where(amax > 0, np.frexp(amax)[1] - 1 + 127, 0) - down, 1)
    scale = np.exp2(byte - 127.0)
    codes = (blocks / scale).astype(np.float32).astype(dtype).astype(np.float64)
    return np.moveaxis((codes * scale).reshape(v.shape), -1, axis)


WIDE = False


def mx_kscale(k):
    if not WIDE:
        return np.ones(k)
    levels = np.array([10, -10, 5, -5, 0])
    if k % 512:
        return np.exp2(np.random.permutation(np.resize(levels, k // 32))).repeat(32)
    a = np.empty((k // 512, 16))
    for p in range(k // 512):
        a[p, :8] = np.random.permutation(np.resize(levels, 8))
        for g in range(8):
            far = levels[np.abs(levels - a[p, g]) >= 10]
            a[p, g + 8] = far[np.random.randint(len(far))]
    return np.exp2(a.ravel()).repeat(32)


BF16 = ml_dtypes.bfloat16


def bf(x):
    return np.asarray(x, np.float32).astype(BF16)


def f64(x):
    return np.asarray(x).astype(np.float64)


E2M1 = np.array([0.0, 0.5, 1.0, 1.5, 2.0, 3.0, 4.0, 6.0, -0.0, -0.5, -1.0, -1.5, -2.0, -3.0, -4.0, -6.0])


def pack_weight(w, fmt):
    k, n = w.shape
    w = f64(bf(w)).reshape(k // 32, 32, n)
    amax = np.abs(w).max(1)
    if fmt == "e4m3":
        byte = np.frexp(amax)[1] - 1 + 127 - 7
    else:
        mant, ex = np.frexp(amax / 6.0)
        byte = np.where(mant > 0.5, ex, ex - 1) + 127
    byte = np.clip(np.where(amax > 0, byte, 1), 1, 254)
    scaled = (w * np.exp2(127.0 - byte)[:, None, :]).reshape(k, n).astype(np.float32)
    by_word = np.ascontiguousarray(scaled.reshape(k // 512, 128, 4, n).transpose(0, 1, 3, 2))
    if fmt == "e4m3":
        words = by_word.astype(ml_dtypes.float8_e4m3fn).view(np.uint8)
    else:
        c = by_word.astype(ml_dtypes.float4_e2m1fn).view(np.uint8) & 0xF
        words = c[..., 0::2] | (c[..., 1::2] << 4)
    return np.ascontiguousarray(words), np.ascontiguousarray(byte.astype(np.uint8).reshape(k // 512, 16, n))


def unpack_weight(words, scales, fmt):
    g, p, n, _ = words.shape
    if fmt == "e4m3":
        vals = np.ascontiguousarray(words).view(ml_dtypes.float8_e4m3fn).astype(np.float64)
    else:
        nib = np.empty((g, p, n, 4), np.uint8)
        nib[..., 0::2] = words & 0xF
        nib[..., 1::2] = words >> 4
        vals = E2M1[nib]
    vals = vals * np.repeat(np.exp2(scales.astype(np.float64) - 127.0), 8, axis=1)[..., None]
    return vals.transpose(0, 1, 3, 2).reshape(g * 512, n)
def pack4(w):
    words, scales = pack_weight(w, "e2m1")
    return words.reshape(words.shape[0], 128, -1), scales


def unpack4(words, scales):
    return unpack_weight(words.reshape(words.shape[0], 128, -1, 2), scales, "e2m1")


def planes(Y):
    n, m = Y.shape
    b = f64(bf(Y)).reshape(n // 32, 32, m)
    amax = np.abs(b).max(1)
    byte = np.clip(np.where(amax > 0, np.frexp(amax)[1] - 1 + 127 - 7, 1), 1, 254)
    codes = (b * np.exp2(127.0 - byte)[:, None, :]).reshape(n, m).astype(np.float32).astype(ml_dtypes.float8_e4m3fn).view(np.uint8)
    words = codes.reshape(n // 512, 128, 4, m).transpose(0, 1, 3, 2)
    return np.ascontiguousarray(words), np.ascontiguousarray(byte.astype(np.uint8).reshape(n // 512, 16, m))


R, K, H, F, D, O = 1024, 1024, 512, 8, 512, 512

def setup_inputs():
    rn = np.random.randn
    s, d, t = mx_kscale(K), mx_kscale(D), mx_kscale(H)
    u = mx_kscale(H)[::H // F]
    c = (F * H) ** -0.25
    x_words, x_scales = pack_weight(rn(K, R) * s[:, None], "e4m3")
    basis_words, basis_scales = pack4(rn(D, F * H) * d[:, None])
    return {
        "x_words": x_words, "x_scales": x_scales,
        "w": bf(rn(K, H) * c / np.sqrt(K) * t[None, :] / s[:, None]),
        "w_bias": bf(0.3 * rn(H) * c * t),
        "fields": bf(rn(R, F) * u[None, :]),
        "basis_words": basis_words, "basis_scales": basis_scales,
        "mix": bf(rn(D, O) * c / np.sqrt(D) / d[:, None]),
        "pair_gain": bf((1 + 0.1 * rn(F, H)) / (u[:, None] * t[None, :])),
        "bias": bf(0.3 * rn(O)),
        "gain": bf(np.exp(0.8 * rn(O))),
    }

def reference(x_words, x_scales, w, w_bias, fields, basis_words, basis_scales, mix, pair_gain, bias, gain):
    a = (unpack_weight(x_words, x_scales, "e4m3").T @ mxq(f64(w), 0, "e4m3")) + f64(w_bias)
    pairs = (f64(fields)[:, :, None] * a[:, None, :]).reshape(R, F * H)
    filters = (unpack4(basis_words, basis_scales).T @ mxq(f64(mix), 0, "e4m3")) * f64(pair_gain).reshape(F * H, 1)
    h = (mxq(pairs, 1, "e4m3") @ mxq(filters, 0, "e4m3")) + f64(bias)
    y = h / (1 + np.exp(-h)) * f64(gain)
    words, scales = planes(y.T)
    return y, words, scales

from contextlib import ExitStack

import concourse.mybir as mybir
from concourse.masks import make_identity

R, K, H, F, D, O = 1024, 1024, 512, 8, 512, 512
FLOPS = 2 * R * K * H + 2 * F * H * D * O + 2 * R * F * H * O

F32 = mybir.dt.float32
BF16 = mybir.dt.bfloat16
I32 = mybir.dt.int32
U32 = mybir.dt.uint32
U8 = mybir.dt.uint8
FP8X4 = mybir.dt.float8_e4m3fn_x4
FP4X4 = mybir.dt.float4_e2m1fn_x4
ALU = mybir.AluOpType
ACT = mybir.ActivationFunctionType

P = 128
ROWS = 512
W_SPLIT = 10
PAIR_SLOTS = 12
GROUP_SLOTS = 3
SCALAR_UNITS = 10
MIX_SPLIT = 0
CHUNKS = ((0, 512), (512, 256), (768, 256))


def tile_cin_pair_filters_k4_kernel(
    tc, x_words, x_scales, w, w_bias, fields, basis_words, basis_scales, mix, pair_gain, bias, gain, out_0, out_1, out_2
):
    nc = tc.nc
    with ExitStack() as ctx:
        sb = ctx.enter_context(tc.tile_pool(name="sb", bufs=1))
        ps = ctx.enter_context(tc.psum_pool(name="ps", bufs=1))
        ctx.enter_context(tc.manual_schedule())

        def tile(name, shape, dtype):
            return sb.tile(shape, dtype, name=name, align_bytes=64)

        banks = [ps.tile([P, 512], F32, name="bank%d" % i) for i in range(8)]
        filter_banks = banks[4:6]
        turn_banks = banks[6:8]
        sum_banks = [[banks[i] for i in ring] for ring in ((0, 1, 2, 3), (4, 5, 0, 1), (2, 3, 4, 5))]
        out_banks = [banks[i] for i in (2, 3, 2, 3, 0, 1, 6, 7)]

        w_raw = tile("w_raw", [P, 2, 4, H], BF16)
        w_grouped = tile("w_grouped", [P, 2, H, 4], BF16)
        w_codes = tile("w_codes", [P, 2, H], U32)
        w_plane = tile("w_plane", [P, 2, H], U8)
        x_codes = tile("x_codes", [P, 2, R], U32)
        x_plane = tile("x_plane", [P, 2, R], U8)
        mix_raw = tile("mix_raw", [P, 4, O], BF16)
        mix_grouped = tile("mix_grouped", [P, O, 4], BF16)
        mix_codes = tile("mix_codes", [P, O], U32)
        mix_plane = tile("mix_plane", [P, O], U8)
        basis_raw = tile("basis_raw", [P, 2 * F * H], U8)
        basis_codes = tile("basis_codes", [P, 2 * F * H], U8)
        basis_plane_raw = tile("basis_plane_raw", [P, F * H], U8)
        basis_plane = tile("basis_plane", [P, F * H], U8)
        maps = tile("maps", [P, R // P, H], F32)
        w_bias_cols = tile("w_bias_cols", [P, 4], BF16)
        w_bias_rows = tile("w_bias_rows", [P, H], F32)
        fields_raw = tile("fields_raw", [P, R // P, 2 * F], BF16)
        fields_f32 = tile("fields_f32", [P, R // P, F], F32)
        pair_gain_raw = tile("pair_gain_raw", [P, H], BF16)
        pair_gain_sorted = tile("pair_gain_sorted", [P, 4, P], BF16)
        pair_gain_cols = tile("pair_gain_cols", [P, F, 4], F32)
        bias_cols = tile("bias_cols", [P, 4], BF16)
        gain_cols = tile("gain_cols", [P, 4], BF16)
        ident_bf16 = tile("ident_bf16", [P, P], BF16)
        ident_f32 = tile("ident_f32", [P, P], F32)
        warm = tile("warm", [P, 2], F32)
        pair_rows = tile("pair_rows", [P, PAIR_SLOTS, H], BF16)
        pair_grouped = tile("pair_grouped", [P, GROUP_SLOTS, ROWS, 4], BF16)
        pair_codes = tile("pair_codes", [P, 2 * F, ROWS], U32)
        pair_plane = tile("pair_plane", [P, 2 * F, ROWS], U8)
        filter_grouped = tile("filter_grouped", [P, GROUP_SLOTS, O, 4], BF16)
        filter_codes = tile("filter_codes", [P, F, O], U32)
        filter_plane = tile("filter_plane", [P, F, O], U8)
        silu = tile("silu", [P, 4, ROWS], F32)
        y_cols = tile("y_cols", [P, 4, R], F32)
        y_grouped = tile("y_grouped", [P, R, 4], BF16)
        y_codes = tile("y_codes", [P, R], U32)
        y_plane = tile("y_plane", [P, R], U8)
        y_rows = tile("y_rows", [P, 4, O], F32)

        def flat(ap):
            return ap.rearrange("p n t -> p (n t)")

        def quantize(codes, plane, grouped):
            nc.vector.quantize_mx(out=codes.bitcast(FP8X4), scales=plane, in_=flat(grouped))

        nc.vector.memset(warm[:], 0.0)
        nc.vector.memset(x_plane[:].rearrange("p g n -> p (g n)").bitcast(I32), 0)
        nc.vector.memset(basis_plane_raw[:].bitcast(I32), 0)
        nc.vector.memset(pair_gain_raw[:], 0.0)
        nc.gpsimd.dma_start(out=w_bias_cols[:], in_=w_bias.rearrange("(p j) -> p j", j=4))
        nc.gpsimd.dma_start(out=fields_raw[:, :, 0:F], in_=fields.rearrange("(b p) f -> p b f", p=P))
        nc.gpsimd.dma_start(out=pair_gain_raw[0:F, :], in_=pair_gain)
        make_identity(nc, ident_bf16[:])
        make_identity(nc, ident_f32[:])

        nc.scalar.activation(out=warm[:, 1:2], in_=warm[:, 0:1], func=ACT.Silu)

        x_src = x_words.rearrange("g p n t -> p g (n t)").bitcast(I32)
        x_rows = x_scales.rearrange("g (q r) n -> r q g n", r=4)
        basis_rows = basis_scales[0].rearrange("(q r) n -> r q n", r=4)

        def load_x(c):
            rows = slice(c * ROWS, (c + 1) * ROWS)
            nc.sync.dma_start(out=x_codes[:, :, rows].bitcast(I32), in_=x_src[:, :, rows])

        def load_basis(lo, hi):
            cols = slice(2 * H * lo, 2 * H * hi)
            nc.sync.dma_start(out=basis_raw[:, cols].bitcast(I32), in_=basis_words[0][:, cols].bitcast(I32))

        for g in range(2):
            nc.sync.dma_start(out=w_raw[:, g], in_=w[512 * g : 512 * (g + 1), :].rearrange("(p j) h -> p j h", j=4))
        for r in range(4):
            nc.sync.dma_start(out=x_plane[r:P:32, :, :].bitcast(I32), in_=x_rows[r].bitcast(I32))
        load_x(0)
        nc.sync.dma_start(out=mix_raw[:], in_=mix.rearrange("(p j) o -> p j o", j=4))
        for r in range(4):
            nc.sync.dma_start(out=basis_plane_raw[r:P:32, :].bitcast(I32), in_=basis_rows[r].bitcast(I32))
        load_basis(0, 2)
        load_x(1)
        load_basis(2, F)
        nc.sync.dma_start(out=bias_cols[:], in_=bias.rearrange("(m s) -> m s", s=4))
        nc.sync.dma_start(out=gain_cols[:], in_=gain.rearrange("(m s) -> m s", s=4))

        small = turn_banks[0][:].bitcast(BF16).rearrange("p (j n) -> p j n", j=8)

        def spread_w_bias():
            for j in range(4):
                nc.tensor.transpose(small[:, j, :], w_bias_cols[:, j : j + 1].to_broadcast([P, P]), ident_bf16[:])
            for u in range(2):
                nc.scalar.copy(
                    out=w_bias_rows[:].rearrange("p (u b i j e) -> p u b i j e", u=2, i=2, j=4, e=2)[:, u],
                    in_=small[:, 0:4, :].rearrange("p j (b u e i) -> p u b i j e", u=2, e=2, i=2)[:, u],
                )

        def turn_pair_gain():
            nc.scalar.copy(
                out=pair_gain_sorted[:].rearrange("p t (b i) -> p t b i", i=8),
                in_=pair_gain_raw[:].rearrange("p (b t i) -> p t b i", t=4, i=8),
            )
            for t in range(4):
                nc.tensor.transpose(small[:, 4 + t, :], pair_gain_sorted[:, t, :], ident_bf16[:])
            nc.scalar.copy(out=pair_gain_cols[:], in_=small[:, 4:8, 0:F].rearrange("p t f -> p f t"))

        def group_w(g):
            src = w_raw[:, g].rearrange("p j (b u x) -> p u b x j", u=2, x=16)
            dst = w_grouped[:, g].rearrange("p (u b x) j -> p u b x j", u=2, x=16)
            nc.vector.tensor_copy(out=dst[:, :, 0:W_SPLIT], in_=src[:, :, 0:W_SPLIT])
            nc.scalar.copy(out=dst[:, :, W_SPLIT:16], in_=src[:, :, W_SPLIT:16])

        def project(b):
            cols = slice(b * P, (b + 1) * P)
            for g in range(2):
                nc.tensor.matmul_mx(
                    out=banks[b % 4][:],
                    lhsT=x_codes[:, g, cols].bitcast(FP8X4),
                    lhsT_scale=x_plane[:, g, cols],
                    rhs=w_codes[:, g, :].bitcast(FP8X4),
                    rhs_scale=w_plane[:, g, :],
                    start=(g == 0),
                    stop=(g == 1),
                )

        def add_w_bias(b):
            nc.vector.tensor_tensor(
                out=maps[:, b, :].rearrange("p (c i e) -> p c i e", i=8, e=2),
                in0=banks[b % 4][:].rearrange("p (c e i) -> p c i e", i=8, e=2),
                in1=w_bias_rows[:].rearrange("p (c i e) -> p c i e", i=8, e=2),
                op=ALU.add,
            )

        def group_mix():
            src = mix_raw[:].rearrange("p j (m s) -> p s m j", s=4)
            dst = mix_grouped[:].rearrange("p (s m) j -> p s m j", s=4)
            nc.vector.tensor_copy(out=dst, in_=src)

        def sort_basis(lo, hi):
            fs = slice(lo, hi)
            for raw, ordered, run in ((basis_raw, basis_codes, 4), (basis_plane_raw, basis_plane, 2)):
                nc.vector.tensor_copy(
                    out=ordered[:].bitcast(I32).rearrange("p (f t b i) -> p f t b i", f=F, t=4, i=run)[:, fs],
                    in_=raw[:].bitcast(I32).rearrange("p (f b t i) -> p f t b i", f=F, t=4, i=run)[:, fs],
                )

        def unit_items(unit):
            if unit < F:
                return [(j, unit) for j in range(4)]
            c, k = divmod(unit - F, 4)
            return [(4 + 2 * c + j % 2, 2 * k + j // 2) for j in range(4)]

        def pair_slot(unit, j):
            return pair_rows[:, (4 * unit + j) % PAIR_SLOTS, :]

        def multiply_pairs(unit, j):
            b, f = unit_items(unit)[j]
            if unit < SCALAR_UNITS:
                nc.scalar.activation(
                    out=pair_slot(unit, j), in_=maps[:, b, :], func=ACT.Copy, scale=fields_f32[:, b, f : f + 1]
                )
            else:
                nc.vector.tensor_scalar(
                    out=pair_slot(unit, j), in0=maps[:, b, :], scalar1=fields_f32[:, b, f : f + 1], scalar2=None, op0=ALU.mult
                )

        def turn_pairs(unit):
            for j in range(4):
                words = pair_slot(unit, j).bitcast(F32)
                bank = turn_banks[j // 2][:].rearrange("p (j u r) -> p j u r", j=2, u=2)
                for u in range(2):
                    nc.tensor.transpose(bank[:, j % 2, u, :], words[:, u * P : (u + 1) * P], ident_f32[:])

        def group_pairs(unit, half):
            words = flat(pair_grouped[:, unit % GROUP_SLOTS]).bitcast(F32)
            nc.scalar.copy(
                out=words.rearrange("p (j r u) -> p j r u", j=4, u=2)[:, 2 * half : 2 * half + 2],
                in_=turn_banks[half][:].rearrange("p (j u r) -> p j r u", j=2, u=2),
            )

        def quantize_pairs(unit):
            quantize(pair_codes[:, unit, :], pair_plane[:, unit, :], pair_grouped[:, unit % GROUP_SLOTS])

        def mix_filters(f, s):
            cols = slice(s * P, (s + 1) * P)
            for t in range(4):
                at = (4 * f + t) * P
                nc.tensor.matmul_mx(
                    out=filter_banks[s % 2][:, t * P : (t + 1) * P],
                    lhsT=basis_codes[:, 2 * at : 2 * (at + P)].bitcast(FP4X4),
                    lhsT_scale=basis_plane[:, at : at + P],
                    rhs=mix_codes[:, cols].bitcast(FP8X4),
                    rhs_scale=mix_plane[:, cols],
                    start=True,
                    stop=True,
                )

        def group_filters(f, s):
            nc.vector.tensor_tensor(
                out=filter_grouped[:, f % GROUP_SLOTS, s * P : (s + 1) * P, :],
                in0=filter_banks[s % 2][:].rearrange("p (t m) -> p m t", t=4),
                in1=pair_gain_cols[:, f : f + 1, :].to_broadcast([P, P, 4]),
                op=ALU.mult,
            )

        def quantize_filters(f):
            quantize(filter_codes[:, f, :], filter_plane[:, f, :], filter_grouped[:, f % GROUP_SLOTS])

        def compress(unit, s):
            if unit < F:
                c, passes = 0, [(unit, slice(0, ROWS))]
            else:
                c, k = divmod(unit - 4, 4)
                passes = [(2 * k, slice(0, 256)), (2 * k + 1, slice(256, 512))]
            cols = slice(s * P, (s + 1) * P)
            for f, rows in passes:
                nc.tensor.matmul_mx(
                    out=sum_banks[c][s][:, 0 : CHUNKS[c][1]],
                    lhsT=filter_codes[:, f, cols].bitcast(FP8X4),
                    lhsT_scale=filter_plane[:, f, cols],
                    rhs=pair_codes[:, unit, rows].bitcast(FP8X4),
                    rhs_scale=pair_plane[:, unit, rows],
                    start=(f == 0),
                    stop=(f == F - 1),
                )

        def chunk_rows(c):
            return slice(CHUNKS[c][0], CHUNKS[c][0] + CHUNKS[c][1])

        def silu_cols(c, s):
            lo = CHUNKS[c][0] % ROWS
            return silu[:, s, lo : lo + CHUNKS[c][1]]

        def activate(c, s):
            nc.scalar.activation(
                out=silu_cols(c, s), in_=sum_banks[c][s][:, 0 : CHUNKS[c][1]], func=ACT.Silu, bias=bias_cols[:, s : s + 1]
            )

        def apply_gain(c, s):
            nc.vector.tensor_scalar(
                out=y_cols[:, s, chunk_rows(c)], in0=silu_cols(c, s), scalar1=gain_cols[:, s : s + 1], scalar2=None, op0=ALU.mult
            )

        def group_y(rows):
            nc.vector.tensor_copy(out=y_grouped[:, rows, :], in_=y_cols[:, :, rows].rearrange("p s r -> p r s"))

        def quantize_y(rows):
            quantize(y_codes[:, rows], y_plane[:, rows], y_grouped[:, rows, :])

        def store_planes(rows):
            words = out_1[0].rearrange("p m t -> p (m t)").bitcast(I32)
            nc.sync.dma_start(out=words[:, rows], in_=y_codes[:, rows].bitcast(I32))
            scale_rows = out_2[0].rearrange("(q r) m -> r q m", r=4)
            for r in range(4):
                nc.sync.dma_start(out=scale_rows[r][:, rows].bitcast(I32), in_=y_plane[r:P:32, rows].bitcast(I32))

        def turn_y(b):
            for s in range(4):
                nc.tensor.transpose(out_banks[b][:, s * P : (s + 1) * P], y_cols[:, s, b * P : (b + 1) * P], ident_f32[:])

        def store_y(b, engine):
            dst = y_rows[:, b % 4, :].rearrange("p (m s) -> p m s", s=4)
            src = out_banks[b][:].rearrange("p (s m) -> p m s", s=4)
            if engine == "scalar":
                nc.scalar.copy(out=dst, in_=src)
            else:
                nc.vector.tensor_copy(out=dst, in_=src)
            nc.sync.dma_start(out=out_0[b * P : (b + 1) * P, :], in_=y_rows[:, b % 4, :])

        group_w(0)
        group_w(1)
        spread_w_bias()
        nc.scalar.copy(out=fields_f32[:], in_=fields_raw[:, :, 0:F])
        turn_pair_gain()
        for g in range(2):
            quantize(w_codes[:, g, :], w_plane[:, g, :], w_grouped[:, g])
        for b in range(4):
            project(b)
            add_w_bias(b)
        for j in range(4):
            multiply_pairs(0, j)
        group_mix()
        sort_basis(0, 2)
        quantize(mix_codes[:], mix_plane[:], mix_grouped[:])
        turn_pairs(0)
        for j in range(4):
            multiply_pairs(1, j)
        mix_filters(0, 0)
        mix_filters(0, 1)

        for f in range(F):
            group_filters(f, 0)
            group_pairs(f, 0)
            if f < 2:
                project(4 + 2 * f)
            group_filters(f, 1)
            mix_filters(f, 2)
            group_pairs(f, 1)
            if f < 2:
                project(5 + 2 * f)
            if f >= 2:
                compress(f - 2, 3)
            mix_filters(f, 3)
            if f >= 1:
                quantize_filters(f - 1)
            if f < 2:
                add_w_bias(4 + 2 * f)
                add_w_bias(5 + 2 * f)
            if f in (0, 2, 4):
                sort_basis(f + 2, f + 4)
            for j in range(4):
                multiply_pairs(f + 2, j)
            turn_pairs(f + 1)
            group_filters(f, 2)
            group_filters(f, 3)
            if f + 1 < F:
                mix_filters(f + 1, 0)
            if f >= 1:
                compress(f - 1, 0)
            if f + 1 < F:
                mix_filters(f + 1, 1)
            if f >= 1:
                compress(f - 1, 1)
                compress(f - 1, 2)
            quantize_pairs(f)
        compress(F - 2, 3)
        quantize_filters(F - 1)
        for s in range(4):
            compress(F - 1, s)

        units = 2 * F
        for unit in range(F, units):
            k = unit - F
            group_pairs(unit, 0)
            group_pairs(unit, 1)
            if k == 4:
                turn_y(2)
                turn_y(3)
            if k in (0, 1):
                activate(0, 2 * k)
                activate(0, 2 * k + 1)
            if k == 3:
                store_y(0, "scalar")
                store_y(1, "scalar")
            if k == 4:
                for s in range(4):
                    activate(1, s)
            if k == 6:
                store_y(4, "scalar")
                store_y(5, "scalar")
            if k in (1, 2):
                apply_gain(0, 2 * k - 2)
                apply_gain(0, 2 * k - 1)
            if k == 5:
                for s in range(4):
                    apply_gain(1, s)
            if unit + 2 < units:
                multiply_pairs(unit + 2, 0)
                multiply_pairs(unit + 2, 1)
            quantize_pairs(unit)
            if k == 4:
                store_y(2, "vector")
                store_y(3, "vector")
            if unit + 2 < units:
                multiply_pairs(unit + 2, 2)
                multiply_pairs(unit + 2, 3)
            if unit + 1 < units:
                turn_pairs(unit + 1)
            if k == 2:
                turn_y(0)
                turn_y(1)
            if k == 5:
                turn_y(4)
                turn_y(5)
            if k in (2, 3):
                group_y(slice((k - 2) * 256, (k - 1) * 256))
            if k == 5:
                quantize_y(chunk_rows(0))
                store_planes(chunk_rows(0))
            if k == 6:
                group_y(chunk_rows(1))
            for s in range(4):
                compress(unit, s)

        quantize_y(chunk_rows(1))
        store_planes(chunk_rows(1))
        for s in range(4):
            activate(2, s)
            apply_gain(2, s)
        turn_y(6)
        turn_y(7)
        group_y(chunk_rows(2))
        store_y(6, "scalar")
        quantize_y(chunk_rows(2))
        store_y(7, "vector")
        store_planes(chunk_rows(2))
